import numpy as np
import ml_dtypes


def mxq(x, axis, fmt="e4m3"):
    dtype, down = {"e4m3": (ml_dtypes.float8_e4m3fn, 7), "e5m2": (ml_dtypes.float8_e5m2, 14)}[fmt]
    v = np.moveaxis(np.asarray(x, np.float32).astype(ml_dtypes.bfloat16).astype(np.float64), axis, -1)
    blocks = v.reshape(v.shape[:-1] + (-1, 32))
    amax = np.abs(blocks).max(-1, keepdims=True)
    byte = np.maximum(np.where(amax > 0, np.frexp(amax)[1] - 1 + 127, 0) - down, 1)
    scale = np.exp2(byte - 127.0)
    codes = (blocks / scale).astype(np.float32).astype(dtype).astype(np.float64)
    return np.moveaxis((codes * scale).reshape(v.shape), -1, axis)


WIDE = False


def mx_kscale(k):
    if not WIDE:
        return np.ones(k)
    levels = np.array([10, -10, 5, -5, 0])
    if k % 512:
        return np.exp2(np.random.permutation(np.resize(levels, k // 32))).repeat(32)
    a = np.empty((k // 512, 16))
    for p in range(k // 512):
        a[p, :8] = np.random.permutation(np.resize(levels, 8))
        for g in range(8):
            far = levels[np.abs(levels - a[p, g]) >= 10]
            a[p, g + 8] = far[np.random.randint(len(far))]
    return np.exp2(a.ravel()).repeat(32)


def f64(x):
    return np.asarray(x).astype(np.float64)


def striped(idx):
    return np.tile(np.asarray(idx).reshape(-1, 16).T, (8, 1)).astype(np.uint16)


def unstriped(offs):
    return offs[:16].T.reshape(-1).astype(np.int64)


O, G, T, D, M = 2, 1024, 4096, 512, 512


def setup_inputs():
    n = np.random.standard_normal
    s = mx_kscale(D)[:, None]
    grid = lambda x: np.round(x * 32) / 32
    return {
        "cb": (grid(n((O, D, T))) / s).astype(np.float32),
        "w": (n((D, M)) * s / np.sqrt(O * D)).astype(np.float32),
        "norm": np.tile(np.random.randint(32, 129, G) / 64.0, (128, 1)).astype(np.float32),
        "bias": (0.3 * n((M, 1))).astype(np.float32),
        "offs": striped(np.random.randint(0, T, O * G)),
    }


def reference(cb, w, norm, bias, offs):
    code = unstriped(offs).reshape(O, G)
    e = sum(f64(cb)[o][:, code[o]] for o in range(O)) * f64(norm)[:1]
    y = mxq(f64(w), 0, "e4m3").T @ mxq(e, 0, "e4m3")
    y = y + f64(bias)
    return y

@@ -1,0 +1,178 @@
+from contextlib import ExitStack
+
+import concourse.mybir as mybir
+from concourse.masks import make_identity
+
+O, D, T, G, M = 2, 512, 4096, 1024, 512
+P = 128
+PACK = 4
+HALF = M // 2
+
+FLOPS = 2 * M * D * G
+BYTES = 4 * (O * D * T + D * M + G + M + M * G) + 2 * 128 * 128
+
+F32 = mybir.dt.float32
+BF16 = mybir.dt.bfloat16
+U32 = mybir.dt.uint32
+U16 = mybir.dt.uint16
+U8 = mybir.dt.uint8
+FP8X4 = mybir.dt.float8_e4m3fn_x4
+IDENTITY = mybir.ActivationFunctionType.Identity
+MULT = mybir.AluOpType.mult
+ADD = mybir.AluOpType.add
+
+PIECES = ((0, 256), (256, 256), (512, 256), (768, 128), (896, 128))
+
+
+def tile_attend_aq_bias_kernel(tc, cb, w, norm, bias, offs, out):
+    nc = tc.nc
+    with ExitStack() as ctx:
+        hold = ctx.enter_context(tc.tile_pool(name="hold", bufs=1))
+        ring = ctx.enter_context(tc.tile_pool(name="ring", bufs=2))
+        psum_setup = ctx.enter_context(tc.psum_pool(name="psum_setup", bufs=1))
+        psum = ctx.enter_context(tc.psum_pool(name="psum", bufs=4))
+
+        offsets = hold.tile([P, O * G // 16], U16, name="offsets")
+        nc.sync.dma_start(offsets[:], offs)
+
+        tables = {}
+
+        def load_table(o, t):
+            table = hold.tile([P, T], F32, name="table_%d_%d" % (o, t))
+            nc.sync.dma_start(table[:], cb[o].rearrange("(p t) c -> p t c", t=PACK)[:, t, :])
+            tables[o, t] = table
+
+        w_raw = [hold.tile([P, PACK, HALF], F32, name="w_raw_%d" % h) for h in range(2)]
+
+        def load_w(h):
+            nc.sync.dma_start(w_raw[h][:], w.rearrange("(p t) m -> p t m", t=PACK)[:, :, h * HALF : (h + 1) * HALF])
+
+        bias_rows = hold.tile([P, P], F32, name="bias_rows")
+        nc.gpsimd.memset(bias_rows[:], 0.0)
+        norm_cols = hold.tile([P, G // P], F32, name="norm_cols")
+
+        load_table(0, 0)
+        nc.sync.dma_start(norm_cols[:], norm[0:1, :].rearrange("o (p c) -> (o p) c", c=G // P))
+        nc.sync.dma_start(bias_rows[0 : M // P, :], bias.rearrange("(b p) o -> b (p o)", p=P))
+        load_table(1, 0)
+        load_table(0, 1)
+        load_table(1, 1)
+        load_w(0)
+        load_table(0, 2)
+        load_table(1, 2)
+        load_table(0, 3)
+        load_table(1, 3)
+        load_w(1)
+
+        ident = hold.tile([P, P], F32, name="ident")
+        make_identity(nc, ident[:])
+
+        norm_all = hold.tile([P, G], F32, name="norm_all")
+        for b in range(2):
+            turned = psum_setup.tile([P, 4, P], F32, name="turned_%d" % b)
+            for c in range(4):
+                nc.tensor.transpose(turned[:, c, :], norm_cols[:, 4 * b + c : 4 * b + c + 1].to_broadcast([P, P]), ident[:])
+            nc.scalar.copy(
+                norm_all[:].rearrange("q (p c) -> q p c", c=8)[:, :, 4 * b : 4 * b + 4],
+                turned[:].rearrange("q c p -> q p c"),
+            )
+        bias_turned = psum_setup.tile([P, P], F32, name="bias_turned")
+        nc.tensor.transpose(bias_turned[:], bias_rows[:], ident[:])
+        bias_cols = hold.tile([P, M // P], F32, name="bias_cols")
+        nc.scalar.copy(bias_cols[:], bias_turned[:, 0 : M // P])
+
+        w_codes = [hold.tile([P, HALF], U32, name="w_codes_%d" % h, align_bytes=64) for h in range(2)]
+        w_scales = [hold.tile([P, HALF], U8, name="w_scales_%d" % h, align_bytes=64) for h in range(2)]
+        w_groups = [hold.tile([P, HALF, PACK], BF16, name="w_groups_%d" % h, align_bytes=64) for h in range(2)]
+
+        def group_w(h):
+            for b in range(2):
+                nc.scalar.copy(
+                    w_groups[h][:, b * P : (b + 1) * P, :],
+                    w_raw[h][:, :, b * P : (b + 1) * P].rearrange("p t m -> p m t"),
+                )
+
+        def quantise_w(h):
+            nc.vector.quantize_mx(
+                out=w_codes[h][:].bitcast(FP8X4),
+                scales=w_scales[h][:],
+                in_=w_groups[h][:].rearrange("p m t -> p (m t)"),
+            )
+
+        e_groups = hold.tile([P, G, PACK], BF16, name="e_groups", align_bytes=64)
+        e_codes = hold.tile([P, G], U32, name="e_codes", align_bytes=64)
+        e_scales = hold.tile([P, G], U8, name="e_scales", align_bytes=64)
+
+        def gather(o, t, dst, g, n):
+            nc.vector.tensor_tensor(
+                dst[:, g : g + n],
+                tables[o, t][:].indirect(offsets[:, (o * G + g) // 16 : (o * G + g + n) // 16]),
+                norm_all[:, g : g + n],
+                MULT,
+            )
+
+        def add(a, b, dst, g, n):
+            nc.vector.tensor_tensor(dst[:, g : g + n], a[:, g : g + n], b[:, g : g + n], ADD)
+
+        def place(src, t, g, n):
+            nc.vector.tensor_copy(e_groups[:, g : g + n, t], src[:, g : g + n])
+
+        for t in range(PACK - 1):
+            first = ring.tile([P, G], F32, name="first")
+            second = ring.tile([P, G], F32, name="second")
+            total = ring.tile([P, G], BF16, name="total")
+            gather(0, t, first, 0, G)
+            gather(1, t, second, 0, G)
+            add(first, second, total, 0, G)
+            place(total, t, 0, G)
+            if t == 1:
+                group_w(0)
+                quantise_w(0)
+
+        last = PACK - 1
+        first = ring.tile([P, G], F32, name="first")
+        second = ring.tile([P, G], F32, name="second")
+        total = ring.tile([P, G], BF16, name="total")
+        gather(0, last, first, 0, G)
+        group_w(1)
+
+        def quantise_e(g, n):
+            nc.vector.quantize_mx(
+                out=e_codes[:, g : g + n].bitcast(FP8X4),
+                scales=e_scales[:, g : g + n],
+                in_=e_groups[:, g : g + n, :].rearrange("p g t -> p (g t)"),
+            )
+
+        def multiply(i, g, n):
+            for h in range(2):
+                result = hold.tile([P, 2, n], F32, name="result_%d_%d" % (i, h))
+                for b in range(2):
+                    acc = psum.tile([P, n], F32, name="acc")
+                    nc.tensor.matmul_mx(
+                        out=acc[:],
+                        lhsT=w_codes[h][:, b * P : (b + 1) * P].bitcast(FP8X4),
+                        lhsT_scale=w_scales[h][:, b * P : (b + 1) * P],
+                        rhs=e_codes[:, g : g + n].bitcast(FP8X4),
+                        rhs_scale=e_scales[:, g : g + n],
+                        start=True,
+                        stop=True,
+                    )
+                    nc.scalar.activation(result[:, b, :], acc[:], IDENTITY, bias=bias_cols[:, 2 * h + b : 2 * h + b + 1])
+                nc.sync.dma_start(
+                    out[h * HALF : (h + 1) * HALF, g : g + n].rearrange("(b p) g -> p b g", b=2),
+                    result[:],
+                )
+
+        steps = len(PIECES) + 3
+        for s in range(steps + 1):
+            if s < len(PIECES):
+                gather(1, last, second, *PIECES[s])
+            if 0 <= s - 2 < len(PIECES):
+                place(total, last, *PIECES[s - 2])
+            if 0 <= s - 1 < len(PIECES):
+                add(first, second, total, *PIECES[s - 1])
+            if 0 <= s - 3 < len(PIECES):
+                quantise_e(*PIECES[s - 3])
+                if s == 3:
+                    quantise_w(1)
+                multiply(s - 3, *PIECES[s - 3])

@@ -21,7 +21,9 @@ IDENTITY = mybir.ActivationFunctionType.Identity
 MULT = mybir.AluOpType.mult
 ADD = mybir.AluOpType.add
 
-PIECES = ((0, 256), (256, 256), (512, 256), (768, 128), (896, 128))
+BATCHES = (((0, 128), (128, 128)), ((256, 256), (512, 256)), ((768, 128), (896, 128)))
+GROUP = 256
+ON_VECTOR = ((768, 0), (768, 1), (768, 2))
 
 
 def tile_attend_aq_bias_kernel(tc, cb, w, norm, bias, offs, out):
@@ -30,7 +32,7 @@ def tile_attend_aq_bias_kernel(tc, cb, w, norm, bias, offs, out):
         hold = ctx.enter_context(tc.tile_pool(name="hold", bufs=1))
         ring = ctx.enter_context(tc.tile_pool(name="ring", bufs=2))
         psum_setup = ctx.enter_context(tc.psum_pool(name="psum_setup", bufs=1))
-        psum = ctx.enter_context(tc.psum_pool(name="psum", bufs=4))
+        psum = ctx.enter_context(tc.psum_pool(name="psum", bufs=5))
 
         offsets = hold.tile([P, O * G // 16], U16, name="offsets")
         nc.sync.dma_start(offsets[:], offs)
@@ -51,9 +53,9 @@ def tile_attend_aq_bias_kernel(tc, cb, w, norm, bias, offs, out):
         nc.gpsimd.memset(bias_rows[:], 0.0)
         norm_cols = hold.tile([P, G // P], F32, name="norm_cols")
 
-        load_table(0, 0)
         nc.sync.dma_start(norm_cols[:], norm[0:1, :].rearrange("o (p c) -> (o p) c", c=G // P))
         nc.sync.dma_start(bias_rows[0 : M // P, :], bias.rearrange("(b p) o -> b (p o)", p=P))
+        load_table(0, 0)
         load_table(1, 0)
         load_table(0, 1)
         load_table(1, 1)
@@ -143,36 +145,45 @@ def tile_attend_aq_bias_kernel(tc, cb, w, norm, bias, offs, out):
                 in_=e_groups[:, g : g + n, :].rearrange("p g t -> p (g t)"),
             )
 
-        def multiply(i, g, n):
-            for h in range(2):
-                result = hold.tile([P, 2, n], F32, name="result_%d_%d" % (i, h))
-                for b in range(2):
-                    acc = psum.tile([P, n], F32, name="acc")
-                    nc.tensor.matmul_mx(
-                        out=acc[:],
-                        lhsT=w_codes[h][:, b * P : (b + 1) * P].bitcast(FP8X4),
-                        lhsT_scale=w_scales[h][:, b * P : (b + 1) * P],
-                        rhs=e_codes[:, g : g + n].bitcast(FP8X4),
-                        rhs_scale=e_scales[:, g : g + n],
-                        start=True,
-                        stop=True,
-                    )
-                    nc.scalar.activation(result[:, b, :], acc[:], IDENTITY, bias=bias_cols[:, 2 * h + b : 2 * h + b + 1])
-                nc.sync.dma_start(
-                    out[h * HALF : (h + 1) * HALF, g : g + n].rearrange("(b p) g -> p b g", b=2),
-                    result[:],
-                )
+        results = [hold.tile([P, 2, G], F32, name="results_%d" % h) for h in range(2)]
 
-        steps = len(PIECES) + 3
-        for s in range(steps + 1):
-            if s < len(PIECES):
-                gather(1, last, second, *PIECES[s])
-            if 0 <= s - 2 < len(PIECES):
-                place(total, last, *PIECES[s - 2])
-            if 0 <= s - 1 < len(PIECES):
-                add(first, second, total, *PIECES[s - 1])
-            if 0 <= s - 3 < len(PIECES):
-                quantise_e(*PIECES[s - 3])
-                if s == 3:
-                    quantise_w(1)
-                multiply(s - 3, *PIECES[s - 3])
+        def multiply(g, h):
+            cols = slice(g, g + GROUP)
+            for b in range(2):
+                block = 2 * h + b
+                acc = psum.tile([P, GROUP], F32, name="acc")
+                nc.tensor.matmul_mx(
+                    out=acc[:],
+                    lhsT=w_codes[h][:, b * P : (b + 1) * P].bitcast(FP8X4),
+                    lhsT_scale=w_scales[h][:, b * P : (b + 1) * P],
+                    rhs=e_codes[:, cols].bitcast(FP8X4),
+                    rhs_scale=e_scales[:, cols],
+                    start=True,
+                    stop=True,
+                )
+                if (g, block) in ON_VECTOR:
+                    nc.vector.tensor_scalar_add(results[h][:, b, cols], acc[:], bias_cols[:, block : block + 1])
+                else:
+                    nc.scalar.activation(results[h][:, b, cols], acc[:], IDENTITY, bias=bias_cols[:, block : block + 1])
+            nc.sync.dma_start(
+                out[h * HALF : (h + 1) * HALF, cols].rearrange("(b p) g -> p b g", b=2), results[h][:, :, cols]
+            )
+
+        for i, batch in enumerate(BATCHES):
+            for piece in batch:
+                gather(1, last, second, *piece)
+            if i == 1:
+                quantise_w(1)
+                multiply(0, 1)
+            for piece in batch:
+                add(first, second, total, *piece)
+            for piece in batch:
+                place(total, last, *piece)
+            for piece in batch:
+                quantise_e(*piece)
+            if i == 0:
+                multiply(0, 0)
+            else:
+                for g in range(batch[0][0], batch[1][0] + batch[1][1], GROUP):
+                    for h in range(2):
+                        multiply(g, h)

@@ -35,7 +35,6 @@ def tile_attend_aq_bias_kernel(tc, cb, w, norm, bias, offs, out):
         psum = ctx.enter_context(tc.psum_pool(name="psum", bufs=5))
 
         offsets = hold.tile([P, O * G // 16], U16, name="offsets")
-        nc.sync.dma_start(offsets[:], offs)
 
         tables = {}
 
@@ -53,9 +52,10 @@ def tile_attend_aq_bias_kernel(tc, cb, w, norm, bias, offs, out):
         nc.gpsimd.memset(bias_rows[:], 0.0)
         norm_cols = hold.tile([P, G // P], F32, name="norm_cols")
 
-        nc.sync.dma_start(norm_cols[:], norm[0:1, :].rearrange("o (p c) -> (o p) c", c=G // P))
-        nc.sync.dma_start(bias_rows[0 : M // P, :], bias.rearrange("(b p) o -> b (p o)", p=P))
+        nc.scalar.dma_start(norm_cols[:], norm[0:1, :].rearrange("o (p c) -> (o p) c", c=G // P))
+        nc.scalar.dma_start(bias_rows[0 : M // P, :], bias.rearrange("(b p) o -> b (p o)", p=P))
         load_table(0, 0)
+        nc.sync.dma_start(offsets[:], offs)
         load_table(1, 0)
         load_table(0, 1)
         load_table(1, 1)
@@ -122,11 +122,11 @@ def tile_attend_aq_bias_kernel(tc, cb, w, norm, bias, offs, out):
         for t in range(PACK - 1):
             first = ring.tile([P, G], F32, name="first")
             second = ring.tile([P, G], F32, name="second")
-            total = ring.tile([P, G], BF16, name="total")
+            total = hold.tile([P, G], BF16, name="total")
             gather(0, t, first, 0, G)
             gather(1, t, second, 0, G)
             add(first, second, total, 0, G)
-            place(total, t, 0, G)
+            nc.scalar.copy(e_groups[:, :, t], total[:])
             if t == 1:
                 group_w(0)
                 quantise_w(0)
@@ -134,7 +134,7 @@ def tile_attend_aq_bias_kernel(tc, cb, w, norm, bias, offs, out):
         last = PACK - 1
         first = ring.tile([P, G], F32, name="first")
         second = ring.tile([P, G], F32, name="second")
-        total = ring.tile([P, G], BF16, name="total")
+        total = hold.tile([P, G], BF16, name="total")
         gather(0, last, first, 0, G)
         group_w(1)
 

@@ -21,9 +21,8 @@ IDENTITY = mybir.ActivationFunctionType.Identity
 MULT = mybir.AluOpType.mult
 ADD = mybir.AluOpType.add
 
-BATCHES = (((0, 128), (128, 128)), ((256, 256), (512, 256)), ((768, 128), (896, 128)))
-GROUP = 256
-ON_VECTOR = ((768, 0), (768, 1), (768, 2))
+PIECES = ((0, 256), (256, 256), (512, 256), (768, 128), (896, 128))
+ON_VECTOR = ((1, 3), (3, 1), (3, 3), (4, 1), (4, 3))
 
 
 def tile_attend_aq_bias_kernel(tc, cb, w, norm, bias, offs, out):
@@ -31,8 +30,7 @@ def tile_attend_aq_bias_kernel(tc, cb, w, norm, bias, offs, out):
     with ExitStack() as ctx:
         hold = ctx.enter_context(tc.tile_pool(name="hold", bufs=1))
         ring = ctx.enter_context(tc.tile_pool(name="ring", bufs=2))
-        psum_setup = ctx.enter_context(tc.psum_pool(name="psum_setup", bufs=1))
-        psum = ctx.enter_context(tc.psum_pool(name="psum", bufs=5))
+        psum = ctx.enter_context(tc.psum_pool(name="psum", bufs=8))
 
         offsets = hold.tile([P, O * G // 16], U16, name="offsets")
 
@@ -59,11 +57,11 @@ def tile_attend_aq_bias_kernel(tc, cb, w, norm, bias, offs, out):
         load_table(1, 0)
         load_table(0, 1)
         load_table(1, 1)
-        load_w(0)
         load_table(0, 2)
         load_table(1, 2)
         load_table(0, 3)
         load_table(1, 3)
+        load_w(0)
         load_w(1)
 
         ident = hold.tile([P, P], F32, name="ident")
@@ -71,14 +69,14 @@ def tile_attend_aq_bias_kernel(tc, cb, w, norm, bias, offs, out):
 
         norm_all = hold.tile([P, G], F32, name="norm_all")
         for b in range(2):
-            turned = psum_setup.tile([P, 4, P], F32, name="turned_%d" % b)
+            turned = psum.tile([P, 4, P], F32, name="turned_%d" % b, tag="bank")
             for c in range(4):
                 nc.tensor.transpose(turned[:, c, :], norm_cols[:, 4 * b + c : 4 * b + c + 1].to_broadcast([P, P]), ident[:])
             nc.scalar.copy(
                 norm_all[:].rearrange("q (p c) -> q p c", c=8)[:, :, 4 * b : 4 * b + 4],
                 turned[:].rearrange("q c p -> q p c"),
             )
-        bias_turned = psum_setup.tile([P, P], F32, name="bias_turned")
+        bias_turned = psum.tile([P, P], F32, name="bias_turned", tag="bank")
         nc.tensor.transpose(bias_turned[:], bias_rows[:], ident[:])
         bias_cols = hold.tile([P, M // P], F32, name="bias_cols")
         nc.scalar.copy(bias_cols[:], bias_turned[:, 0 : M // P])
@@ -87,12 +85,13 @@ def tile_attend_aq_bias_kernel(tc, cb, w, norm, bias, offs, out):
         w_scales = [hold.tile([P, HALF], U8, name="w_scales_%d" % h, align_bytes=64) for h in range(2)]
         w_groups = [hold.tile([P, HALF, PACK], BF16, name="w_groups_%d" % h, align_bytes=64) for h in range(2)]
 
-        def group_w(h):
-            for b in range(2):
-                nc.scalar.copy(
-                    w_groups[h][:, b * P : (b + 1) * P, :],
-                    w_raw[h][:, :, b * P : (b + 1) * P].rearrange("p t m -> p m t"),
-                )
+        def group_w(block):
+            h, b = divmod(block, 2)
+            copy = nc.vector.tensor_copy if block == 0 else nc.scalar.copy
+            copy(
+                w_groups[h][:, b * P : (b + 1) * P, :],
+                w_raw[h][:, :, b * P : (b + 1) * P].rearrange("p t m -> p m t"),
+            )
 
         def quantise_w(h):
             nc.vector.quantize_mx(
@@ -127,16 +126,12 @@ def tile_attend_aq_bias_kernel(tc, cb, w, norm, bias, offs, out):
             gather(1, t, second, 0, G)
             add(first, second, total, 0, G)
             nc.scalar.copy(e_groups[:, :, t], total[:])
-            if t == 1:
-                group_w(0)
-                quantise_w(0)
 
         last = PACK - 1
         first = ring.tile([P, G], F32, name="first")
         second = ring.tile([P, G], F32, name="second")
         total = hold.tile([P, G], BF16, name="total")
         gather(0, last, first, 0, G)
-        group_w(1)
 
         def quantise_e(g, n):
             nc.vector.quantize_mx(
@@ -147,11 +142,12 @@ def tile_attend_aq_bias_kernel(tc, cb, w, norm, bias, offs, out):
 
         results = [hold.tile([P, 2, G], F32, name="results_%d" % h) for h in range(2)]
 
-        def multiply(g, h):
-            cols = slice(g, g + GROUP)
+        def multiply(i, h):
+            g, n = PIECES[i]
+            cols = slice(g, g + n)
             for b in range(2):
                 block = 2 * h + b
-                acc = psum.tile([P, GROUP], F32, name="acc")
+                acc = psum.tile([P, n], F32, name="acc", tag="bank")
                 nc.tensor.matmul_mx(
                     out=acc[:],
                     lhsT=w_codes[h][:, b * P : (b + 1) * P].bitcast(FP8X4),
@@ -161,7 +157,7 @@ def tile_attend_aq_bias_kernel(tc, cb, w, norm, bias, offs, out):
                     start=True,
                     stop=True,
                 )
-                if (g, block) in ON_VECTOR:
+                if (i, block) in ON_VECTOR:
                     nc.vector.tensor_scalar_add(results[h][:, b, cols], acc[:], bias_cols[:, block : block + 1])
                 else:
                     nc.scalar.activation(results[h][:, b, cols], acc[:], IDENTITY, bias=bias_cols[:, block : block + 1])
@@ -169,21 +165,53 @@ def tile_attend_aq_bias_kernel(tc, cb, w, norm, bias, offs, out):
                 out[h * HALF : (h + 1) * HALF, cols].rearrange("(b p) g -> p b g", b=2), results[h][:, :, cols]
             )
 
-        for i, batch in enumerate(BATCHES):
-            for piece in batch:
-                gather(1, last, second, *piece)
-            if i == 1:
-                quantise_w(1)
-                multiply(0, 1)
-            for piece in batch:
-                add(first, second, total, *piece)
-            for piece in batch:
-                place(total, last, *piece)
-            for piece in batch:
-                quantise_e(*piece)
-            if i == 0:
-                multiply(0, 0)
-            else:
-                for g in range(batch[0][0], batch[1][0] + batch[1][1], GROUP):
-                    for h in range(2):
-                        multiply(g, h)
+        def gather_last(i):
+            gather(1, last, second, *PIECES[i])
+
+        def add_last(i):
+            add(first, second, total, *PIECES[i])
+
+        def place_last(i):
+            g, n = PIECES[i]
+            copy = nc.scalar.copy if i == 0 else nc.vector.tensor_copy
+            copy(e_groups[:, g : g + n, last], total[:, g : g + n])
+
+        def quantise_last(i):
+            quantise_e(*PIECES[i])
+
+        gather_last(0)
+        gather_last(1)
+        add_last(0)
+        group_w(1)
+        place_last(0)
+        group_w(2)
+        group_w(3)
+        group_w(0)
+        add_last(1)
+        gather_last(2)
+        quantise_w(0)
+        quantise_last(0)
+        multiply(0, 0)
+        place_last(1)
+        add_last(2)
+        quantise_last(1)
+        multiply(1, 0)
+        quantise_w(1)
+        multiply(0, 1)
+        place_last(2)
+        gather_last(3)
+        quantise_last(2)
+        multiply(1, 1)
+        add_last(3)
+        gather_last(4)
+        place_last(3)
+        add_last(4)
+        quantise_last(3)
+        multiply(2, 0)
+        multiply(2, 1)
+        place_last(4)
+        quantise_last(4)
+        multiply(3, 0)
+        multiply(3, 1)
+        multiply(4, 0)
+        multiply(4, 1)

from contextlib import ExitStack

import concourse.mybir as mybir
from concourse.masks import make_identity

O, D, T, G, M = 2, 512, 4096, 1024, 512
P = 128
PACK = 4
HALF = M // 2

FLOPS = 2 * M * D * G
BYTES = 4 * (O * D * T + D * M + G + M + M * G) + 2 * 128 * 128

F32 = mybir.dt.float32
BF16 = mybir.dt.bfloat16
U32 = mybir.dt.uint32
U16 = mybir.dt.uint16
U8 = mybir.dt.uint8
FP8X4 = mybir.dt.float8_e4m3fn_x4
IDENTITY = mybir.ActivationFunctionType.Identity
MULT = mybir.AluOpType.mult
ADD = mybir.AluOpType.add

PIECES = ((0, 256), (256, 256), (512, 256), (768, 128), (896, 128))
ON_VECTOR = ((1, 3), (3, 1), (3, 3), (4, 1), (4, 3))


def tile_attend_aq_bias_kernel(tc, cb, w, norm, bias, offs, out):
    nc = tc.nc
    with ExitStack() as ctx:
        hold = ctx.enter_context(tc.tile_pool(name="hold", bufs=1))
        ring = ctx.enter_context(tc.tile_pool(name="ring", bufs=2))
        psum = ctx.enter_context(tc.psum_pool(name="psum", bufs=8))

        offsets = hold.tile([P, O * G // 16], U16, name="offsets")

        tables = {}

        def load_table(o, t):
            table = hold.tile([P, T], F32, name="table_%d_%d" % (o, t))
            nc.sync.dma_start(table[:], cb[o].rearrange("(p t) c -> p t c", t=PACK)[:, t, :])
            tables[o, t] = table

        w_raw = [hold.tile([P, PACK, HALF], F32, name="w_raw_%d" % h) for h in range(2)]

        def load_w(h):
            nc.sync.dma_start(w_raw[h][:], w.rearrange("(p t) m -> p t m", t=PACK)[:, :, h * HALF : (h + 1) * HALF])

        bias_rows = hold.tile([P, P], F32, name="bias_rows")
        nc.gpsimd.memset(bias_rows[:], 0.0)
        norm_cols = hold.tile([P, G // P], F32, name="norm_cols")

        nc.scalar.dma_start(norm_cols[:], norm[0:1, :].rearrange("o (p c) -> (o p) c", c=G // P))
        nc.scalar.dma_start(bias_rows[0 : M // P, :], bias.rearrange("(b p) o -> b (p o)", p=P))
        load_table(0, 0)
        nc.sync.dma_start(offsets[:], offs)
        load_table(1, 0)
        load_table(0, 1)
        load_table(1, 1)
        load_table(0, 2)
        load_table(1, 2)
        load_table(0, 3)
        load_table(1, 3)
        load_w(0)
        load_w(1)

        ident = hold.tile([P, P], F32, name="ident")
        make_identity(nc, ident[:])

        norm_all = hold.tile([P, G], F32, name="norm_all")
        for b in range(2):
            turned = psum.tile([P, 4, P], F32, name="turned_%d" % b, tag="bank")
            for c in range(4):
                nc.tensor.transpose(turned[:, c, :], norm_cols[:, 4 * b + c : 4 * b + c + 1].to_broadcast([P, P]), ident[:])
            nc.scalar.copy(
                norm_all[:].rearrange("q (p c) -> q p c", c=8)[:, :, 4 * b : 4 * b + 4],
                turned[:].rearrange("q c p -> q p c"),
            )
        bias_turned = psum.tile([P, P], F32, name="bias_turned", tag="bank")
        nc.tensor.transpose(bias_turned[:], bias_rows[:], ident[:])
        bias_cols = hold.tile([P, M // P], F32, name="bias_cols")
        nc.scalar.copy(bias_cols[:], bias_turned[:, 0 : M // P])

        w_codes = [hold.tile([P, HALF], U32, name="w_codes_%d" % h, align_bytes=64) for h in range(2)]
        w_scales = [hold.tile([P, HALF], U8, name="w_scales_%d" % h, align_bytes=64) for h in range(2)]
        w_groups = [hold.tile([P, HALF, PACK], BF16, name="w_groups_%d" % h, align_bytes=64) for h in range(2)]

        def group_w(block):
            h, b = divmod(block, 2)
            copy = nc.vector.tensor_copy if block == 0 else nc.scalar.copy
            copy(
                w_groups[h][:, b * P : (b + 1) * P, :],
                w_raw[h][:, :, b * P : (b + 1) * P].rearrange("p t m -> p m t"),
            )

        def quantise_w(h):
            nc.vector.quantize_mx(
                out=w_codes[h][:].bitcast(FP8X4),
                scales=w_scales[h][:],
                in_=w_groups[h][:].rearrange("p m t -> p (m t)"),
            )

        e_groups = hold.tile([P, G, PACK], BF16, name="e_groups", align_bytes=64)
        e_codes = hold.tile([P, G], U32, name="e_codes", align_bytes=64)
        e_scales = hold.tile([P, G], U8, name="e_scales", align_bytes=64)

        def gather(o, t, dst, g, n):
            nc.vector.tensor_tensor(
                dst[:, g : g + n],
                tables[o, t][:].indirect(offsets[:, (o * G + g) // 16 : (o * G + g + n) // 16]),
                norm_all[:, g : g + n],
                MULT,
            )

        def add(a, b, dst, g, n):
            nc.vector.tensor_tensor(dst[:, g : g + n], a[:, g : g + n], b[:, g : g + n], ADD)

        def place(src, t, g, n):
            nc.vector.tensor_copy(e_groups[:, g : g + n, t], src[:, g : g + n])

        for t in range(PACK - 1):
            first = ring.tile([P, G], F32, name="first")
            second = ring.tile([P, G], F32, name="second")
            total = hold.tile([P, G], BF16, name="total")
            gather(0, t, first, 0, G)
            gather(1, t, second, 0, G)
            add(first, second, total, 0, G)
            nc.scalar.copy(e_groups[:, :, t], total[:])

        last = PACK - 1
        first = ring.tile([P, G], F32, name="first")
        second = ring.tile([P, G], F32, name="second")
        total = hold.tile([P, G], BF16, name="total")
        gather(0, last, first, 0, G)

        def quantise_e(g, n):
            nc.vector.quantize_mx(
                out=e_codes[:, g : g + n].bitcast(FP8X4),
                scales=e_scales[:, g : g + n],
                in_=e_groups[:, g : g + n, :].rearrange("p g t -> p (g t)"),
            )

        results = [hold.tile([P, 2, G], F32, name="results_%d" % h) for h in range(2)]

        def multiply(i, h):
            g, n = PIECES[i]
            cols = slice(g, g + n)
            for b in range(2):
                block = 2 * h + b
                acc = psum.tile([P, n], F32, name="acc", tag="bank")
                nc.tensor.matmul_mx(
                    out=acc[:],
                    lhsT=w_codes[h][:, b * P : (b + 1) * P].bitcast(FP8X4),
                    lhsT_scale=w_scales[h][:, b * P : (b + 1) * P],
                    rhs=e_codes[:, cols].bitcast(FP8X4),
                    rhs_scale=e_scales[:, cols],
                    start=True,
                    stop=True,
                )
                if (i, block) in ON_VECTOR:
                    nc.vector.tensor_scalar_add(results[h][:, b, cols], acc[:], bias_cols[:, block : block + 1])
                else:
                    nc.scalar.activation(results[h][:, b, cols], acc[:], IDENTITY, bias=bias_cols[:, block : block + 1])
            nc.sync.dma_start(
                out[h * HALF : (h + 1) * HALF, cols].rearrange("(b p) g -> p b g", b=2), results[h][:, :, cols]
            )

        def gather_last(i):
            gather(1, last, second, *PIECES[i])

        def add_last(i):
            add(first, second, total, *PIECES[i])

        def place_last(i):
            g, n = PIECES[i]
            copy = nc.scalar.copy if i == 0 else nc.vector.tensor_copy
            copy(e_groups[:, g : g + n, last], total[:, g : g + n])

        def quantise_last(i):
            quantise_e(*PIECES[i])

        gather_last(0)
        gather_last(1)
        add_last(0)
        group_w(1)
        place_last(0)
        group_w(2)
        group_w(3)
        group_w(0)
        add_last(1)
        gather_last(2)
        quantise_w(0)
        quantise_last(0)
        multiply(0, 0)
        place_last(1)
        add_last(2)
        quantise_last(1)
        multiply(1, 0)
        quantise_w(1)
        multiply(0, 1)
        place_last(2)
        gather_last(3)
        quantise_last(2)
        multiply(1, 1)
        add_last(3)
        gather_last(4)
        place_last(3)
        add_last(4)
        quantise_last(3)
        multiply(2, 0)
        multiply(2, 1)
        place_last(4)
        quantise_last(4)
        multiply(3, 0)
        multiply(3, 1)
        multiply(4, 0)
        multiply(4, 1)
